import numpy as np
import ml_dtypes


def mxq(x, axis, fmt="e4m3"):
    dtype, down = {"e4m3": (ml_dtypes.float8_e4m3fn, 7), "e5m2": (ml_dtypes.float8_e5m2, 14)}[fmt]
    v = np.moveaxis(np.asarray(x, np.float32).astype(ml_dtypes.bfloat16).astype(np.float64), axis, -1)
    blocks = v.reshape(v.shape[:-1] + (-1, 32))
    amax = np.abs(blocks).max(-1, keepdims=True)
    byte = np.maximum(np.where(amax > 0, np.frexp(amax)[1] - 1 + 127, 0) - down, 1)
    scale = np.exp2(byte - 127.0)
    codes = (blocks / scale).astype(np.float32).astype(dtype).astype(np.float64)
    return np.moveaxis((codes * scale).reshape(v.shape), -1, axis)


WIDE = False


def mx_kscale(k, group=512):
    if not WIDE:
        return np.ones(k)
    levels = np.array([18, -18])
    if group != 512:
        return np.exp2(np.random.permutation(np.resize(levels, k // group))).repeat(group)
    if k % 512:
        return np.exp2(np.random.permutation(np.resize(levels, k // 32))).repeat(32)
    a = np.empty((k // 512, 16))
    for p in range(k // 512):
        a[p, :8] = np.random.permutation(np.resize(levels, 8))
        for g in range(8):
            far = levels[np.abs(levels - a[p, g]) >= 10]
            a[p, g + 8] = far[np.random.randint(len(far))]
    return np.exp2(a.ravel()).repeat(32)


def f64(x):
    return np.asarray(x).astype(np.float64)


def silu(v):
    return v / (1.0 + np.exp(-v))


def sigmoid(v):
    return 1.0 / (1.0 + np.exp(-v))


G, D, M, F, O, N = 4, 128, 128, 128, 128, 512


def sgn(shape):
    return np.random.uniform(0.5, 2.0, shape) * np.where(np.random.standard_normal(shape) < 0, -1.0, 1.0)


def setup_inputs():
    n = np.random.standard_normal
    s_d = mx_kscale(D, 0)
    s_f = mx_kscale(F, 0)
    return {
        "x": (n((G, D, N)) * s_d[:, None]).astype(np.float32),
        "w": (n((G, D, M)) / np.sqrt(D) / s_d[:, None]).astype(np.float32),
        "hs": (sgn((G, M, 1)) * np.tile(s_f.reshape(F // G, G).T, (1, G))[:, :, None]).astype(np.float32),
        "v": (n((G, F, O)) / np.sqrt(F) / s_f[:, None]).astype(np.float32),
        "og": (n((G, O, N))).astype(np.float32),
    }


def reference(x, w, hs, v, og):
    wq = mxq(f64(w), 1, "e4m3")
    xq = mxq(f64(x), 1, "e4m3")
    z = wq.transpose(0, 2, 1) @ xq
    h = silu(z) * f64(hs)
    u = h.reshape(G * M, N).reshape(G, M, N).transpose(1, 0, 2).reshape(G, M, N)
    vq = mxq(f64(v), 1, "e4m3")
    uq = mxq(u, 1, "e4m3")
    y = vq.transpose(0, 2, 1) @ uq
    a = y * sigmoid(f64(og))
    return a

@@ -1,0 +1,176 @@
+from contextlib import ExitStack
+
+import concourse.mybir as mybir
+
+G, D, N = 4, 128, 512
+P = 128
+ROWS = 32
+PACK = 4
+W = 128
+CHUNKS = N // W
+FLOPS = 2 * 2 * G * D * D * N
+
+F32 = mybir.dt.float32
+BF16 = mybir.dt.bfloat16
+U32 = mybir.dt.uint32
+U8 = mybir.dt.uint8
+FP8X4 = mybir.dt.float8_e4m3fn_x4
+ACT = mybir.ActivationFunctionType
+ALU = mybir.AluOpType
+
+X_LOADS = [[0],[1],[2],[3]]
+OG_LOADS = [[[0,1,2,3],[0,1]],[[0,1,2,3],[2,3]]]
+GATE_BY_GROUP = True
+LOAD_ORDER = ["x0","w","x1","x2","hs","x3","v","og0","og1"]
+STORES = [[[0,1,2],[0]],[[0,1,2],[1]],[[0,1,2],[2]],[[0,1,2],[3]],[[3],[0,1]],[[3],[2,3]]]
+ON_SCALAR = ["v"]
+Z_BANK = [1,0,1,1]
+Y_BANK = [1,1,1,0]
+ORDER = "il:x0 il:w q:x0 q:w il:x1 m1:0 q:x1 m1:1 il:x2 si:0 q:x2 si:1 il:x3 m1:2 mul:0 q:x3 mul:1 si:2 m1:3 il:v q:u0 mul:2 si:3 q:v q:u1 th:0 th:1 q:u2 m2:0 m2:1 mul:3 q:u3 m2:2 o:012_0 m2:3 th:2 St:0 th:3 o:012_1 St:1 o:012_2 St:2 o:3_0 o:3_1 St:4 o:012_3 St:3 o:3_2 o:3_3 St:5".split()
+
+
+def tile_rows_monarch_silu_gate_kernel(tc, x, w, hs, v, og, out):
+    nc = tc.nc
+    with ExitStack() as ctx:
+        sb = ctx.enter_context(tc.tile_pool(name="sb", bufs=1))
+        ps = ctx.enter_context(tc.psum_pool(name="ps", bufs=1))
+        ctx.enter_context(tc.manual_schedule())
+
+        banks = [[ps.tile([P, N], F32, name="bank%d%d" % (b, g)) for g in range(G)] for b in range(2)]
+
+        warm_in = sb.tile([P, 1], F32, name="warm_in")
+        warm_out = sb.tile([P, 1], F32, name="warm_out")
+        nc.vector.memset(warm_in[:], 0.0)
+        nc.scalar.activation(out=warm_out[:], in_=warm_in[:], func=ACT.Silu)
+
+        raw = {}
+        gate_in = {}
+        hs_t = sb.tile([P, G, 8], F32, name="hs_t")
+        x_rows = x.rearrange("g (p j) n -> (g p) j n", j=PACK)
+        og_rows = og.rearrange("g o n -> o g n")
+        out_rows = out.rearrange("g o n -> o g n")
+        for name in LOAD_ORDER:
+            if name == "w" or name == "v":
+                src = w if name == "w" else v
+                t = sb.tile([P, PACK, W], F32, name="raw_" + name)
+                nc.sync.dma_start(out=t[:], in_=src.rearrange("g (p j) m -> (g p) j m", j=PACK))
+                raw[name] = t[:]
+            elif name == "hs":
+                with nc.allow_non_contiguous_dma(reason="one scale to a partition and group"):
+                    nc.sync.dma_start(out=hs_t[:, :, 0:1], in_=hs.rearrange("g m o -> m g o"))
+            elif name[0] == "x":
+                cs = X_LOADS[int(name[1])]
+                t = sb.tile([P, PACK, W * len(cs)], F32, name="raw_" + name)
+                nc.sync.dma_start(out=t[:], in_=x_rows[:, :, cs[0] * W : (cs[-1] + 1) * W])
+                for i, c in enumerate(cs):
+                    raw["x%d" % c] = t[:, :, i * W : (i + 1) * W]
+            else:
+                cs, gs = OG_LOADS[int(name[2])]
+                t = sb.tile([P, len(gs), W * len(cs)], F32, name="raw_" + name)
+                nc.sync.dma_start(out=t[:], in_=og_rows[:, gs[0] : gs[-1] + 1, cs[0] * W : (cs[-1] + 1) * W])
+                if GATE_BY_GROUP:
+                    for j, g in enumerate(gs):
+                        gate_in[g] = t[:, j, :]
+                else:
+                    for i, c in enumerate(cs):
+                        gate_in[c] = t[:, :, i * W : (i + 1) * W]
+
+        res = {}
+        store_tiles = []
+        for k, (cs, gs) in enumerate(STORES):
+            t = sb.tile([P, len(gs), W * len(cs)], F32, name="res%d" % k)
+            store_tiles.append(t)
+            for i, c in enumerate(cs):
+                for j, g in enumerate(gs):
+                    res[(c, g)] = (t, j, cs[0])
+
+        words = {}
+        codes = {}
+        scales = {}
+        act = {}
+        half_gate = {}
+
+        def src_order(ap):
+            return ap.rearrange("p j (c i) -> p c j i", i=4)
+
+        def dst_order(t):
+            return t[:].rearrange("p (c i) j -> p c j i", i=4)
+
+        def interleave(name):
+            t = sb.tile([P, W, PACK], BF16, name="words_" + name, align_bytes=64)
+            words[name] = t
+            src, dst = src_order(raw[name]), dst_order(t)
+            if name == "v":
+                if name in ON_SCALAR:
+                    nc.scalar.activation(out=dst, in_=src, func=ACT.Copy, scale=0.5)
+                else:
+                    nc.vector.tensor_scalar(out=dst, in0=src, scalar1=0.5, scalar2=None, op0=ALU.mult)
+            elif name in ON_SCALAR:
+                nc.scalar.copy(out=dst, in_=src)
+            else:
+                nc.vector.tensor_copy(out=dst, in_=src)
+
+        def quantize(name):
+            codes[name] = sb.tile([P, W], U32, name="codes_" + name, align_bytes=64)
+            scales[name] = sb.tile([P, W], U8, name="scales_" + name, align_bytes=64)
+            nc.vector.quantize_mx(
+                out=codes[name][:].bitcast(FP8X4),
+                scales=scales[name][:],
+                in_=words[name][:].rearrange("p n j -> p (n j)"),
+            )
+
+        def product(bank, c, weights, moving):
+            for g in range(G):
+                rows = slice(ROWS * g, ROWS * (g + 1))
+                nc.tensor.matmul_mx(
+                    out=banks[bank][g][:, c * W : (c + 1) * W],
+                    lhsT=codes[weights][rows, :].bitcast(FP8X4),
+                    lhsT_scale=scales[weights][rows, :],
+                    rhs=codes[moving][rows, :].bitcast(FP8X4),
+                    rhs_scale=scales[moving][rows, :],
+                    start=True,
+                    stop=True,
+                )
+
+        for job in ORDER:
+            kind, arg = job.split(":")
+            if kind == "il":
+                interleave(arg)
+            elif kind == "q":
+                quantize(arg)
+            elif kind == "m1":
+                product(Z_BANK[int(arg)], int(arg), "w", "x" + arg)
+            elif kind == "m2":
+                product(Y_BANK[int(arg)], int(arg), "v", "u" + arg)
+            elif kind == "si":
+                c = int(arg)
+                act[c] = sb.tile([P, G, W], F32, name="act%d" % c)
+                for g in range(G):
+                    nc.scalar.activation(out=act[c][:, g, :], in_=banks[Z_BANK[c]][g][:, c * W : (c + 1) * W], func=ACT.Silu)
+            elif kind == "mul":
+                c = int(arg)
+                t = sb.tile([P, W, PACK], BF16, name="words_u%d" % c, align_bytes=64)
+                words["u" + arg] = t
+                factor = hs_t[:, :, 0:1].unsqueeze(1).to_broadcast([P, W // 4, G, 4])
+                nc.vector.tensor_tensor(out=dst_order(t), in0=src_order(act[c][:]), in1=factor, op=ALU.mult)
+            elif kind == "th":
+                c = int(arg)
+                half_gate[c] = sb.tile([P, N] if GATE_BY_GROUP else [P, G, W], F32, name="gate%d" % c)
+                nc.scalar.activation(out=half_gate[c][:], in_=gate_in[c], func=ACT.Tanh, scale=0.5)
+            elif kind == "o":
+                cols, g = arg.split("_")
+                g, c, last = int(g), int(cols[0]), int(cols[-1]) + 1
+                t, j, first = res[(c, g)]
+                nc.vector.scalar_tensor_tensor(
+                    out=t[:, j, (c - first) * W : (last - first) * W],
+                    in0=half_gate[g][:, c * W : last * W] if GATE_BY_GROUP else half_gate[c][:, g, :],
+                    scalar=1.0,
+                    in1=banks[Y_BANK[c]][g][:, c * W : last * W],
+                    op0=ALU.add,
+                    op1=ALU.mult,
+                )
+            else:
+                cs, gs = STORES[int(arg)]
+                nc.sync.dma_start(
+                    out=out_rows[:, gs[0] : gs[-1] + 1, cs[0] * W : (cs[-1] + 1) * W], in_=store_tiles[int(arg)][:]
+                )

@@ -21,12 +21,13 @@ ALU = mybir.AluOpType
 X_LOADS = [[0],[1],[2],[3]]
 OG_LOADS = [[[0,1,2,3],[0,1]],[[0,1,2,3],[2,3]]]
 GATE_BY_GROUP = True
-LOAD_ORDER = ["x0","w","x1","x2","hs","x3","v","og0","og1"]
+SPLIT = 80
+LOAD_ORDER = ["x0","w","hs","x1","x2","x3","v","og0","og1"]
 STORES = [[[0,1,2],[0]],[[0,1,2],[1]],[[0,1,2],[2]],[[0,1,2],[3]],[[3],[0,1]],[[3],[2,3]]]
 ON_SCALAR = ["v"]
 Z_BANK = [1,0,1,1]
 Y_BANK = [1,1,1,0]
-ORDER = "il:x0 il:w q:x0 q:w il:x1 m1:0 q:x1 m1:1 il:x2 si:0 q:x2 si:1 il:x3 m1:2 mul:0 q:x3 mul:1 si:2 m1:3 il:v q:u0 mul:2 si:3 q:v q:u1 th:0 th:1 q:u2 m2:0 m2:1 mul:3 q:u3 m2:2 o:012_0 m2:3 th:2 St:0 th:3 o:012_1 St:1 o:012_2 St:2 o:3_0 o:3_1 St:4 o:012_3 St:3 o:3_2 o:3_3 St:5".split()
+ORDER = "il:x0 q:x0 ils:w q:w il:x1 m1:0 q:x1 m1:1 il:x2 tr:0 si:0 q:x2 si:1 il:x3 m1:2 mul:0 q:x3 mul:1 si:2 m1:3 il:v q:u0 mul:2 si:3 q:v q:u1 th:0 th:1 q:u2 m2:0 m2:1 mul:3 m2:2 q:u3 o:012_0 m2:3 th:2 St:0 th:3 o:012_1 St:1 o:012_2 St:2 o:012_3 St:3 o:3_0 o:3_1 St:4 o:3_2 o:3_3 St:5".split()
 
 
 def tile_rows_monarch_silu_gate_kernel(tc, x, w, hs, v, og, out):
@@ -45,7 +46,9 @@ def tile_rows_monarch_silu_gate_kernel(tc, x, w, hs, v, og, out):
 
         raw = {}
         gate_in = {}
-        hs_t = sb.tile([P, G, 8], F32, name="hs_t")
+        hs_rows = sb.tile([P, ROWS], F32, name="hs_rows", align_bytes=64)
+        hs_t = sb.tile([P, ROWS], F32, name="hs_t", align_bytes=64)
+        nc.vector.memset(hs_rows[:], 0.0)
         x_rows = x.rearrange("g (p j) n -> (g p) j n", j=PACK)
         og_rows = og.rearrange("g o n -> o g n")
         out_rows = out.rearrange("g o n -> o g n")
@@ -56,8 +59,7 @@ def tile_rows_monarch_silu_gate_kernel(tc, x, w, hs, v, og, out):
                 nc.sync.dma_start(out=t[:], in_=src.rearrange("g (p j) m -> (g p) j m", j=PACK))
                 raw[name] = t[:]
             elif name == "hs":
-                with nc.allow_non_contiguous_dma(reason="one scale to a partition and group"):
-                    nc.sync.dma_start(out=hs_t[:, :, 0:1], in_=hs.rearrange("g m o -> m g o"))
+                nc.sync.dma_start(out=hs_rows[0:P:8, :], in_=hs.rearrange("g (q r) o -> q g (r o)", q=G))
             elif name[0] == "x":
                 cs = X_LOADS[int(name[1])]
                 t = sb.tile([P, PACK, W * len(cs)], F32, name="raw_" + name)
@@ -94,12 +96,12 @@ def tile_rows_monarch_silu_gate_kernel(tc, x, w, hs, v, og, out):
             return ap.rearrange("p j (c i) -> p c j i", i=4)
 
         def dst_order(t):
-            return t[:].rearrange("p (c i) j -> p c j i", i=4)
+            return t.rearrange("p (c i) j -> p c j i", i=4)
 
         def interleave(name):
             t = sb.tile([P, W, PACK], BF16, name="words_" + name, align_bytes=64)
             words[name] = t
-            src, dst = src_order(raw[name]), dst_order(t)
+            src, dst = src_order(raw[name]), dst_order(t[:])
             if name == "v":
                 if name in ON_SCALAR:
                     nc.scalar.activation(out=dst, in_=src, func=ACT.Copy, scale=0.5)
@@ -136,6 +138,13 @@ def tile_rows_monarch_silu_gate_kernel(tc, x, w, hs, v, og, out):
             kind, arg = job.split(":")
             if kind == "il":
                 interleave(arg)
+            elif kind == "tr":
+                nc.vector.transpose(out=hs_t[:], in_=hs_rows[:])
+            elif kind == "ils":
+                t = sb.tile([P, W, PACK], BF16, name="words_" + arg, align_bytes=64)
+                words[arg] = t
+                nc.vector.tensor_copy(out=dst_order(t[:, 0:SPLIT, :]), in_=src_order(raw[arg][:, :, 0:SPLIT]))
+                nc.scalar.copy(out=dst_order(t[:, SPLIT:W, :]), in_=src_order(raw[arg][:, :, SPLIT:W]))
             elif kind == "q":
                 quantize(arg)
             elif kind == "m1":
@@ -151,8 +160,8 @@ def tile_rows_monarch_silu_gate_kernel(tc, x, w, hs, v, og, out):
                 c = int(arg)
                 t = sb.tile([P, W, PACK], BF16, name="words_u%d" % c, align_bytes=64)
                 words["u" + arg] = t
-                factor = hs_t[:, :, 0:1].unsqueeze(1).to_broadcast([P, W // 4, G, 4])
-                nc.vector.tensor_tensor(out=dst_order(t), in0=src_order(act[c][:]), in1=factor, op=ALU.mult)
+                factor = hs_t[:, 0:ROWS:8].unsqueeze(2).unsqueeze(1).to_broadcast([P, W // 4, G, 4])
+                nc.vector.tensor_tensor(out=dst_order(t[:]), in0=src_order(act[c][:]), in1=factor, op=ALU.mult)
             elif kind == "th":
                 c = int(arg)
                 half_gate[c] = sb.tile([P, N] if GATE_BY_GROUP else [P, G, W], F32, name="gate%d" % c)

from contextlib import ExitStack

import concourse.mybir as mybir

G, D, N = 4, 128, 512
P = 128
ROWS = 32
PACK = 4
W = 128
CHUNKS = N // W
FLOPS = 2 * 2 * G * D * D * N

F32 = mybir.dt.float32
BF16 = mybir.dt.bfloat16
U32 = mybir.dt.uint32
U8 = mybir.dt.uint8
FP8X4 = mybir.dt.float8_e4m3fn_x4
ACT = mybir.ActivationFunctionType
ALU = mybir.AluOpType

X_LOADS = [[0],[1],[2],[3]]
OG_LOADS = [[[0,1,2,3],[0,1]],[[0,1,2,3],[2,3]]]
GATE_BY_GROUP = True
SPLIT = 80
LOAD_ORDER = ["x0","w","hs","x1","x2","x3","v","og0","og1"]
STORES = [[[0,1,2],[0]],[[0,1,2],[1]],[[0,1,2],[2]],[[0,1,2],[3]],[[3],[0,1]],[[3],[2,3]]]
ON_SCALAR = ["v"]
Z_BANK = [1,0,1,1]
Y_BANK = [1,1,1,0]
ORDER = "il:x0 q:x0 ils:w q:w il:x1 m1:0 q:x1 m1:1 il:x2 tr:0 si:0 q:x2 si:1 il:x3 m1:2 mul:0 q:x3 mul:1 si:2 m1:3 il:v q:u0 mul:2 si:3 q:v q:u1 th:0 th:1 q:u2 m2:0 m2:1 mul:3 m2:2 q:u3 o:012_0 m2:3 th:2 St:0 th:3 o:012_1 St:1 o:012_2 St:2 o:012_3 St:3 o:3_0 o:3_1 St:4 o:3_2 o:3_3 St:5".split()


def tile_rows_monarch_silu_gate_kernel(tc, x, w, hs, v, og, out):
    nc = tc.nc
    with ExitStack() as ctx:
        sb = ctx.enter_context(tc.tile_pool(name="sb", bufs=1))
        ps = ctx.enter_context(tc.psum_pool(name="ps", bufs=1))
        ctx.enter_context(tc.manual_schedule())

        banks = [[ps.tile([P, N], F32, name="bank%d%d" % (b, g)) for g in range(G)] for b in range(2)]

        warm_in = sb.tile([P, 1], F32, name="warm_in")
        warm_out = sb.tile([P, 1], F32, name="warm_out")
        nc.vector.memset(warm_in[:], 0.0)
        nc.scalar.activation(out=warm_out[:], in_=warm_in[:], func=ACT.Silu)

        raw = {}
        gate_in = {}
        hs_rows = sb.tile([P, ROWS], F32, name="hs_rows", align_bytes=64)
        hs_t = sb.tile([P, ROWS], F32, name="hs_t", align_bytes=64)
        nc.vector.memset(hs_rows[:], 0.0)
        x_rows = x.rearrange("g (p j) n -> (g p) j n", j=PACK)
        og_rows = og.rearrange("g o n -> o g n")
        out_rows = out.rearrange("g o n -> o g n")
        for name in LOAD_ORDER:
            if name == "w" or name == "v":
                src = w if name == "w" else v
                t = sb.tile([P, PACK, W], F32, name="raw_" + name)
                nc.sync.dma_start(out=t[:], in_=src.rearrange("g (p j) m -> (g p) j m", j=PACK))
                raw[name] = t[:]
            elif name == "hs":
                nc.sync.dma_start(out=hs_rows[0:P:8, :], in_=hs.rearrange("g (q r) o -> q g (r o)", q=G))
            elif name[0] == "x":
                cs = X_LOADS[int(name[1])]
                t = sb.tile([P, PACK, W * len(cs)], F32, name="raw_" + name)
                nc.sync.dma_start(out=t[:], in_=x_rows[:, :, cs[0] * W : (cs[-1] + 1) * W])
                for i, c in enumerate(cs):
                    raw["x%d" % c] = t[:, :, i * W : (i + 1) * W]
            else:
                cs, gs = OG_LOADS[int(name[2])]
                t = sb.tile([P, len(gs), W * len(cs)], F32, name="raw_" + name)
                nc.sync.dma_start(out=t[:], in_=og_rows[:, gs[0] : gs[-1] + 1, cs[0] * W : (cs[-1] + 1) * W])
                if GATE_BY_GROUP:
                    for j, g in enumerate(gs):
                        gate_in[g] = t[:, j, :]
                else:
                    for i, c in enumerate(cs):
                        gate_in[c] = t[:, :, i * W : (i + 1) * W]

        res = {}
        store_tiles = []
        for k, (cs, gs) in enumerate(STORES):
            t = sb.tile([P, len(gs), W * len(cs)], F32, name="res%d" % k)
            store_tiles.append(t)
            for i, c in enumerate(cs):
                for j, g in enumerate(gs):
                    res[(c, g)] = (t, j, cs[0])

        words = {}
        codes = {}
        scales = {}
        act = {}
        half_gate = {}

        def src_order(ap):
            return ap.rearrange("p j (c i) -> p c j i", i=4)

        def dst_order(t):
            return t.rearrange("p (c i) j -> p c j i", i=4)

        def interleave(name):
            t = sb.tile([P, W, PACK], BF16, name="words_" + name, align_bytes=64)
            words[name] = t
            src, dst = src_order(raw[name]), dst_order(t[:])
            if name == "v":
                if name in ON_SCALAR:
                    nc.scalar.activation(out=dst, in_=src, func=ACT.Copy, scale=0.5)
                else:
                    nc.vector.tensor_scalar(out=dst, in0=src, scalar1=0.5, scalar2=None, op0=ALU.mult)
            elif name in ON_SCALAR:
                nc.scalar.copy(out=dst, in_=src)
            else:
                nc.vector.tensor_copy(out=dst, in_=src)

        def quantize(name):
            codes[name] = sb.tile([P, W], U32, name="codes_" + name, align_bytes=64)
            scales[name] = sb.tile([P, W], U8, name="scales_" + name, align_bytes=64)
            nc.vector.quantize_mx(
                out=codes[name][:].bitcast(FP8X4),
                scales=scales[name][:],
                in_=words[name][:].rearrange("p n j -> p (n j)"),
            )

        def product(bank, c, weights, moving):
            for g in range(G):
                rows = slice(ROWS * g, ROWS * (g + 1))
                nc.tensor.matmul_mx(
                    out=banks[bank][g][:, c * W : (c + 1) * W],
                    lhsT=codes[weights][rows, :].bitcast(FP8X4),
                    lhsT_scale=scales[weights][rows, :],
                    rhs=codes[moving][rows, :].bitcast(FP8X4),
                    rhs_scale=scales[moving][rows, :],
                    start=True,
                    stop=True,
                )

        for job in ORDER:
            kind, arg = job.split(":")
            if kind == "il":
                interleave(arg)
            elif kind == "tr":
                nc.vector.transpose(out=hs_t[:], in_=hs_rows[:])
            elif kind == "ils":
                t = sb.tile([P, W, PACK], BF16, name="words_" + arg, align_bytes=64)
                words[arg] = t
                nc.vector.tensor_copy(out=dst_order(t[:, 0:SPLIT, :]), in_=src_order(raw[arg][:, :, 0:SPLIT]))
                nc.scalar.copy(out=dst_order(t[:, SPLIT:W, :]), in_=src_order(raw[arg][:, :, SPLIT:W]))
            elif kind == "q":
                quantize(arg)
            elif kind == "m1":
                product(Z_BANK[int(arg)], int(arg), "w", "x" + arg)
            elif kind == "m2":
                product(Y_BANK[int(arg)], int(arg), "v", "u" + arg)
            elif kind == "si":
                c = int(arg)
                act[c] = sb.tile([P, G, W], F32, name="act%d" % c)
                for g in range(G):
                    nc.scalar.activation(out=act[c][:, g, :], in_=banks[Z_BANK[c]][g][:, c * W : (c + 1) * W], func=ACT.Silu)
            elif kind == "mul":
                c = int(arg)
                t = sb.tile([P, W, PACK], BF16, name="words_u%d" % c, align_bytes=64)
                words["u" + arg] = t
                factor = hs_t[:, 0:ROWS:8].unsqueeze(2).unsqueeze(1).to_broadcast([P, W // 4, G, 4])
                nc.vector.tensor_tensor(out=dst_order(t[:]), in0=src_order(act[c][:]), in1=factor, op=ALU.mult)
            elif kind == "th":
                c = int(arg)
                half_gate[c] = sb.tile([P, N] if GATE_BY_GROUP else [P, G, W], F32, name="gate%d" % c)
                nc.scalar.activation(out=half_gate[c][:], in_=gate_in[c], func=ACT.Tanh, scale=0.5)
            elif kind == "o":
                cols, g = arg.split("_")
                g, c, last = int(g), int(cols[0]), int(cols[-1]) + 1
                t, j, first = res[(c, g)]
                nc.vector.scalar_tensor_tensor(
                    out=t[:, j, (c - first) * W : (last - first) * W],
                    in0=half_gate[g][:, c * W : last * W] if GATE_BY_GROUP else half_gate[c][:, g, :],
                    scalar=1.0,
                    in1=banks[Y_BANK[c]][g][:, c * W : last * W],
                    op0=ALU.add,
                    op1=ALU.mult,
                )
            else:
                cs, gs = STORES[int(arg)]
                nc.sync.dma_start(
                    out=out_rows[:, gs[0] : gs[-1] + 1, cs[0] * W : (cs[-1] + 1) * W], in_=store_tiles[int(arg)][:]
                )
